import numpy as np, ml_dtypes
CORES = [25,29,65,69,153,157,193,197]
N = 8
KB, QP = 1, 32
MEM = [4,5]
def setup_inputs(rng):
    q = rng.standard_normal((N, 128, QP), dtype=np.float32) / 4; k = rng.standard_normal((N, 128, KB * 128), dtype=np.float32)
    a = 2 * np.pi * rng.random((N, QP)); s = 400 * rng.random((N, QP)) ** 1.5; q[:, 0, :] = s * np.cos(a); q[:, 1, :] = s * np.sin(a); q[:, 2, :] = 150 * rng.standard_normal((N, QP)); k[:, 2, :] = 1 + k[:, 2, :] / 50
    c = np.zeros(N); c[MEM] = rng.permutation(len(MEM))
    a = (2 * np.pi * rng.random() + np.pi / 2 * (c.reshape(N, 1, 1) + 0.5) / len(MEM) - 0.5 + (np.arange(KB).reshape(1, KB, 1) + rng.random((N, KB, 128))) / KB).reshape(N, KB * 128); k[:, 0, :] = np.cos(a); k[:, 1, :] = np.sin(a)
    return {"q": q.astype(ml_dtypes.bfloat16), "k": k.astype(ml_dtypes.bfloat16), "v": rng.standard_normal((N, 128, KB * 128), dtype=np.float32).astype(ml_dtypes.bfloat16)}
def setup_inputs_big(rng):
    d = setup_inputs(rng)
    for k in ("v",): d[k] = (d[k].astype(np.float32) * 1048576.0).astype(d[k].dtype)
    return d
def setup_inputs_small(rng):
    d = setup_inputs(rng)
    for k in ("v",): d[k] = (d[k].astype(np.float32) * (1 / 1048576.0)).astype(d[k].dtype)
    return d
def reference(q, k, v):
    Q, K, V = q.astype(np.float64), k.astype(np.float64), v.astype(np.float64)
    y = np.zeros((N, QP, 128))
    for r in range(N):
        js = list(MEM)
        S = np.concatenate([K[j].T @ Q[r] for j in js], axis=0)
        P = np.exp(S - S.max(axis=0)); P = P / P.sum(axis=0)
        y[r] = P.T @ np.concatenate([V[j][:, 128 * b:128 * b + 128] for j in js for b in range(KB)], axis=0)
    return {"y": y.astype(ml_dtypes.bfloat16)}

@@ -1,0 +1,176 @@
+from concourse.bass import DstId, RemoteDMATransfer
+from concourse.mybir import AluOpType, AxisListType, ActivationFunctionType
+
+SIM_CORES = 256
+QP = 32
+W = 256
+
+SCRATCH = {
+    "kvd": ("dram", [128, W], "bfloat16"),
+    "kv": ("sbuf", [128, 2 * W], "bfloat16"),
+    "qz": ("sbuf", [128, 3 * QP], "bfloat16"),
+    "zero": ("sbuf", [128, 128], "bfloat16"),
+    "ones": ("sbuf", [128, 128], "bfloat16"),
+    "eye2": ("sbuf", [128, 2 * QP], "bfloat16"),
+    "dg2": ("sbuf", [128, 2 * QP], "bfloat16"),
+    "negm": ("sbuf", [128, 1], "float32"),
+    "rl": ("sbuf", [128, 1], "float32"),
+    "p": ("sbuf", [128, 2 * QP], "bfloat16"),
+    "yt": ("sbuf", [128, 128], "bfloat16"),
+    "ps_st": ("psum", [128, 512], "float32"),
+    "ps_s": ("psum", [128, 512], "float32"),
+    "ps_l": ("psum", [128, 512], "float32"),
+    "ps_o": ("psum", [128, 512], "float32"),
+}
+SEMAPHORES = ["ld", "staged", "sent", "kv0", "kv1", "q", "zero", "qz0", "eye1", "eye", "ones",
+              "st", "m", "dg", "s", "p", "l", "o", "rl", "y", "stored"]
+
+
+def _place(topo, c):
+    return (topo.host(c), topo.chip(c))
+
+
+def _plan(T, topo):
+    cores = list(T.cores)
+    routes = []
+    for j in T.tables["MEM"]:
+        src = cores[j]
+        idle = [w for w in range(SIM_CORES)
+                if _place(topo, w) == _place(topo, src) and topo.die(w) == topo.die(src) and w not in cores]
+        near, away = [], {}
+        for d in cores:
+            if d == src:
+                continue
+            if _place(topo, d) == _place(topo, src):
+                near.append(d)
+            else:
+                away.setdefault(_place(topo, d), []).append(d)
+
+        def able(ds):
+            return [w for w in idle if all(topo.may_write(w, d) for d in ds)]
+        relays = []
+        for ds in sorted(away.values(), key=lambda ds: len(able(ds))):
+            w = able(ds)[0]
+            idle.remove(w)
+            relays.append((w, ds))
+        routes.append((src, relays, near))
+    return routes
+
+
+def _share(topo, src, dsts):
+    allowed = topo.mask(src, dsts[0])
+    for d in dsts:
+        allowed &= topo.mask(src, d)
+    bits = [1 << b for b in range(allowed.bit_length()) if (allowed >> b) & 1]
+    n = 1
+    while 2 * n * len(dsts) <= len(bits):
+        n *= 2
+    return [sum(bits[i * n:(i + 1) * n]) for i in range(len(dsts))], n
+
+
+def _dst(topo, d, src):
+    rid, pid = topo.addr(d, src)
+    return DstId(rid=rid, pnc=pid)
+
+
+def rank_program(g, core, T, topo):
+    sem = T.sem
+    routes = _plan(T, topo)
+
+    for s, (src, relays, near) in enumerate(routes):
+        for w, ds in relays:
+            if w != core:
+                continue
+            g.wait_ge(sem.staged, _share(topo, src, [r for r, _ in relays] + near)[1])
+            masks, n = _share(topo, core, ds)
+            g.remote_dma_fused(
+                [RemoteDMATransfer(dst_ids=[_dst(topo, d, core)], dma_engine_mask=m, remote_sem=sem["kv%d" % s],
+                                   src=T.kvd[:, :], dst=T.kv[:, W * s:W * s + W]) for d, m in zip(ds, masks)],
+                local_sem=sem.sent)
+            g.wait_ge(sem.sent, n * len(ds))
+            return
+
+    if T.rank_of(core) is None:
+        return
+
+    own = [s for s, r in enumerate(routes) if r[0] == core]
+
+    if own:
+        g.sync.dma_start(T.kvd[:, 0:128], T.k[:, :]).then_inc(sem.ld, 16)
+        g.scalar.dma_start(T.kvd[:, 128:W], T.v[:, :]).then_inc(sem.ld, 16)
+    g.sync.dma_start(T.qz[:, 0:QP], T.q[:, :]).then_inc(sem.q, 16)
+    g.scalar.dma_start(T.qz[:, 2 * QP:3 * QP], T.q[:, :]).then_inc(sem.q, 16)
+    if own:
+        o = W * own[0]
+        g.sync.dma_start(T.kv[:, o:o + 128], T.k[:, :]).then_inc(sem["kv%d" % own[0]], 16)
+        g.scalar.dma_start(T.kv[:, o + 128:o + W], T.v[:, :]).then_inc(sem["kv%d" % own[0]], 16)
+
+    g.vector.memset(T.zero[:, :], 0.0).then_inc(sem.zero, 1)
+    g.vector.memset(T.eye2[0:QP, :], 1.0).then_inc(sem.eye1, 1)
+    g.vector.memset(T.qz[:, QP:2 * QP], 0.0).then_inc(sem.qz0, 1)
+    g.scalar.wait_ge(sem.zero, 1)
+    g.scalar.activation(T.ones[:, :], T.zero[:, :], ActivationFunctionType.Exp).then_inc(sem.ones, 1)
+    g.wait_ge(sem.eye1, 1)
+    g.affine_select(T.eye2[0:QP, :], T.eye2[0:QP, :], [[0, 2], [-1, QP]], AluOpType.is_equal, 0.0, 0, 1).then_inc(sem.eye, 1)
+
+    if own:
+        src, relays, near = routes[own[0]]
+        to = [r for r, _ in relays] + near
+        masks, n = _share(topo, core, to)
+        g.wait_ge(sem.ld, 32)
+        trs = []
+        for d, m in zip(to, masks):
+            if d in near:
+                trs.append(RemoteDMATransfer(dst_ids=[_dst(topo, d, core)], dma_engine_mask=m,
+                                             remote_sem=sem["kv%d" % own[0]], src=T.kvd[:, :],
+                                             dst=T.kv[:, W * own[0]:W * own[0] + W]))
+            else:
+                trs.append(RemoteDMATransfer(dst_ids=[_dst(topo, d, core)], dma_engine_mask=m, remote_sem=sem.staged,
+                                             src=T.kvd[:, :], dst=T.kvd[:, :]))
+        g.remote_dma_fused(trs, local_sem=sem.sent)
+        g.wait_ge(sem.sent, n * len(to))
+
+    need = []
+    for s, (src, relays, near) in enumerate(routes):
+        if src == core:
+            need.append(32)
+        elif core in near:
+            need.append(_share(topo, src, [r for r, _ in relays] + near)[1])
+        else:
+            need.append([_share(topo, w, ds)[1] for w, ds in relays if core in ds][0])
+
+    pe, ve, ac = g.tensor, g.vector, g.scalar
+    pe.wait_ge(sem.q, 32)
+    pe.wait_ge(sem.qz0, 1)
+    for s in range(2):
+        k = T.kv[:, W * s:W * s + 128]
+        pe.wait_ge(sem["kv%d" % s], need[s])
+        pe.matmul(T.ps_st[0:QP, 128 * s:128 * s + 128], T.qz[:, 0:QP], k, start=True, stop=True).then_inc(sem.st, 1)
+        pe.matmul(T.ps_s[:, 0:2 * QP], k, T.qz[:, QP * s:QP * s + 2 * QP], start=(s == 0), stop=False).then_inc(sem.s, 1)
+
+    ve.wait_ge(sem.st, 2)
+    ve.tensor_reduce(T.negm[0:QP, 0:1], T.ps_st[0:QP, 0:256], AxisListType.X, AluOpType.max, negate=True).then_inc(sem.m, 1)
+    ve.wait_ge(sem.m, 1)
+    ve.wait_ge(sem.eye, 1)
+    ve.tensor_scalar(T.dg2[0:QP, :], T.eye2[0:QP, :], T.negm[0:QP, 0:1], None, AluOpType.mult).then_inc(sem.dg, 1)
+
+    pe.wait_ge(sem.dg, 1)
+    pe.wait_ge(sem.ones, 1)
+    pe.matmul(T.ps_s[:, 0:2 * QP], T.ones[0:QP, 0:128], T.dg2[0:QP, :], start=False, stop=True).then_inc(sem.s, 1)
+    ac.wait_ge(sem.s, 3)
+    ac.activation(T.p[:, :], T.ps_s[:, 0:2 * QP], ActivationFunctionType.Exp).then_inc(sem.p, 1)
+    pe.wait_ge(sem.p, 1)
+    for s in range(2):
+        pe.matmul(T.ps_l[0:QP, 0:1], T.p[:, QP * s:QP * s + QP], T.ones[:, 0:1], start=(s == 0), stop=(s == 1)).then_inc(sem.l, 1)
+    for s in range(2):
+        pe.matmul(T.ps_o[0:QP, 0:128], T.p[:, QP * s:QP * s + QP], T.kv[:, W * s + 128:W * s + W],
+                  start=(s == 0), stop=(s == 1)).then_inc(sem.o, 1)
+    ve.wait_ge(sem.l, 2)
+    ve.reciprocal(T.rl[0:QP, 0:1], T.ps_l[0:QP, 0:1]).then_inc(sem.rl, 1)
+    ve.wait_ge(sem.rl, 1)
+    ve.wait_ge(sem.o, 2)
+    ve.tensor_scalar(T.yt[0:QP, :], T.ps_o[0:QP, 0:128], T.rl[0:QP, 0:1], None, AluOpType.mult).then_inc(sem.y, 1)
+
+    g.sync.wait_ge(sem.y, 1)
+    g.sync.dma_start(T.y[:, :], T.yt[0:QP, :]).then_inc(sem.stored, 16)
+    g.sync.wait_ge(sem.stored, 16)

@@ -6,6 +6,8 @@ QP = 32
 W = 256
 
 SCRATCH = {
+    "kd": ("dram", [128, 128], "bfloat16"),
+    "vd": ("dram", [128, 128], "bfloat16"),
     "kvd": ("dram", [128, W], "bfloat16"),
     "kv": ("sbuf", [128, 2 * W], "bfloat16"),
     "qz": ("sbuf", [128, 3 * QP], "bfloat16"),
@@ -22,7 +24,7 @@ SCRATCH = {
     "ps_l": ("psum", [128, 512], "float32"),
     "ps_o": ("psum", [128, 512], "float32"),
 }
-SEMAPHORES = ["ld", "staged", "sent", "kv0", "kv1", "q", "zero", "qz0", "eye1", "eye", "ones",
+SEMAPHORES = ["ld1", "ld2", "staged", "sent", "k0", "k1", "v0", "v1", "q", "zero", "qz0", "eye1", "eye", "ones",
               "st", "m", "dg", "s", "p", "l", "o", "rl", "y", "stored"]
 
 
@@ -30,42 +32,50 @@ def _place(topo, c):
     return (topo.host(c), topo.chip(c))
 
 
+def _count(mask):
+    return bin(mask).count("1")
+
+
 def _plan(T, topo):
     cores = list(T.cores)
     routes = []
     for j in T.tables["MEM"]:
         src = cores[j]
-        idle = [w for w in range(SIM_CORES)
-                if _place(topo, w) == _place(topo, src) and topo.die(w) == topo.die(src) and w not in cores]
-        near, away = [], {}
+        idle = [w for w in range(SIM_CORES) if w not in cores and topo.die(w) == topo.die(src)]
+        near = [d for d in cores if d != src and _place(topo, d) == _place(topo, src)]
+        direct = [d for d in cores if _place(topo, d) != _place(topo, src) and topo.may_write(src, d)]
+        far = {}
         for d in cores:
-            if d == src:
-                continue
-            if _place(topo, d) == _place(topo, src):
-                near.append(d)
-            else:
-                away.setdefault(_place(topo, d), []).append(d)
-
-        def able(ds):
-            return [w for w in idle if all(topo.may_write(w, d) for d in ds)]
+            if not topo.may_write(src, d):
+                far.setdefault(_place(topo, d), []).append(d)
         relays = []
-        for ds in sorted(away.values(), key=lambda ds: len(able(ds))):
-            w = able(ds)[0]
-            idle.remove(w)
-            relays.append((w, ds))
-        routes.append((src, relays, near))
+        for ds in far.values():
+            able = [w for w in idle if all(topo.may_write(w, d) for d in ds)]
+            wk = [w for w in able if _place(topo, w) == _place(topo, src)][0]
+            wv = [w for w in able if all(topo.mates(w, d) for d in ds) and topo.may_write(src, w)][0]
+            idle.remove(wk)
+            idle.remove(wv)
+            relays.append((wk, wv, ds))
+        routes.append((src, relays, direct, near))
     return routes
 
 
-def _share(topo, src, dsts):
-    allowed = topo.mask(src, dsts[0])
-    for d in dsts:
-        allowed &= topo.mask(src, d)
-    bits = [1 << b for b in range(allowed.bit_length()) if (allowed >> b) & 1]
-    n = 1
-    while 2 * n * len(dsts) <= len(bits):
-        n *= 2
-    return [sum(bits[i * n:(i + 1) * n]) for i in range(len(dsts))], n
+def _engines(topo, route):
+    src, relays, direct, near = route
+    every = _count(topo.mask(src, near[0]))
+    out = _count(topo.mask(src, direct[0]))
+    wk, wv, ds = relays[0]
+    return out // len(relays), out // len(direct), (every - out) // len(near), _count(topo.mask(wk, ds[0])) // len(ds)
+
+
+def _deal(topo, src, wants):
+    used, out = 0, {}
+    for d, n in sorted(wants, key=lambda x: _count(topo.mask(src, x[0]))):
+        m = topo.mask(src, d) & ~used
+        bits = [1 << b for b in range(m.bit_length()) if (m >> b) & 1][0:n]
+        out[d] = sum(bits)
+        used |= out[d]
+    return out
 
 
 def _dst(topo, d, src):
@@ -77,17 +87,18 @@ def rank_program(g, core, T, topo):
     sem = T.sem
     routes = _plan(T, topo)
 
-    for s, (src, relays, near) in enumerate(routes):
-        for w, ds in relays:
-            if w != core:
+    for s, route in enumerate(routes):
+        for wk, wv, ds in route[1]:
+            if core not in (wk, wv):
                 continue
-            g.wait_ge(sem.staged, _share(topo, src, [r for r, _ in relays] + near)[1])
-            masks, n = _share(topo, core, ds)
+            n = _engines(topo, route)
+            piece, off, name = (T.kd, W * s, "k%d" % s) if core == wk else (T.vd, W * s + 128, "v%d" % s)
+            g.wait_ge(sem.staged, n[0])
+            masks = _deal(topo, core, [(d, n[3]) for d in ds])
             g.remote_dma_fused(
-                [RemoteDMATransfer(dst_ids=[_dst(topo, d, core)], dma_engine_mask=m, remote_sem=sem["kv%d" % s],
-                                   src=T.kvd[:, :], dst=T.kv[:, W * s:W * s + W]) for d, m in zip(ds, masks)],
-                local_sem=sem.sent)
-            g.wait_ge(sem.sent, n * len(ds))
+                [RemoteDMATransfer(dst_ids=[_dst(topo, d, core)], dma_engine_mask=masks[d], remote_sem=sem[name],
+                                   src=piece[:, :], dst=T.kv[:, off:off + 128]) for d in ds], local_sem=sem.sent)
+            g.wait_ge(sem.sent, n[3] * len(ds))
             return
 
     if T.rank_of(core) is None:
@@ -96,14 +107,16 @@ def rank_program(g, core, T, topo):
     own = [s for s, r in enumerate(routes) if r[0] == core]
 
     if own:
-        g.sync.dma_start(T.kvd[:, 0:128], T.k[:, :]).then_inc(sem.ld, 16)
-        g.scalar.dma_start(T.kvd[:, 128:W], T.v[:, :]).then_inc(sem.ld, 16)
+        g.sync.dma_start(T.kd[:, :], T.k[:, :]).then_inc(sem.ld1, 16)
+        g.scalar.dma_start(T.vd[:, :], T.v[:, :]).then_inc(sem.ld1, 16)
+        g.sync.dma_start(T.kvd[:, 0:128], T.k[:, :]).then_inc(sem.ld2, 16)
+        g.scalar.dma_start(T.kvd[:, 128:W], T.v[:, :]).then_inc(sem.ld2, 16)
     g.sync.dma_start(T.qz[:, 0:QP], T.q[:, :]).then_inc(sem.q, 16)
     g.scalar.dma_start(T.qz[:, 2 * QP:3 * QP], T.q[:, :]).then_inc(sem.q, 16)
     if own:
         o = W * own[0]
-        g.sync.dma_start(T.kv[:, o:o + 128], T.k[:, :]).then_inc(sem["kv%d" % own[0]], 16)
-        g.scalar.dma_start(T.kv[:, o + 128:o + W], T.v[:, :]).then_inc(sem["kv%d" % own[0]], 16)
+        g.sync.dma_start(T.kv[:, o:o + 128], T.k[:, :]).then_inc(sem["k%d" % own[0]], 16)
+        g.scalar.dma_start(T.kv[:, o + 128:o + W], T.v[:, :]).then_inc(sem["v%d" % own[0]], 16)
 
     g.vector.memset(T.zero[:, :], 0.0).then_inc(sem.zero, 1)
     g.vector.memset(T.eye2[0:QP, :], 1.0).then_inc(sem.eye1, 1)
@@ -114,37 +127,42 @@ def rank_program(g, core, T, topo):
     g.affine_select(T.eye2[0:QP, :], T.eye2[0:QP, :], [[0, 2], [-1, QP]], AluOpType.is_equal, 0.0, 0, 1).then_inc(sem.eye, 1)
 
     if own:
-        src, relays, near = routes[own[0]]
-        to = [r for r, _ in relays] + near
-        masks, n = _share(topo, core, to)
-        g.wait_ge(sem.ld, 32)
-        trs = []
-        for d, m in zip(to, masks):
-            if d in near:
-                trs.append(RemoteDMATransfer(dst_ids=[_dst(topo, d, core)], dma_engine_mask=m,
-                                             remote_sem=sem["kv%d" % own[0]], src=T.kvd[:, :],
-                                             dst=T.kv[:, W * own[0]:W * own[0] + W]))
-            else:
-                trs.append(RemoteDMATransfer(dst_ids=[_dst(topo, d, core)], dma_engine_mask=m, remote_sem=sem.staged,
-                                             src=T.kvd[:, :], dst=T.kvd[:, :]))
-        g.remote_dma_fused(trs, local_sem=sem.sent)
-        g.wait_ge(sem.sent, n * len(to))
+        s = own[0]
+        src, relays, direct, near = routes[s]
+        n_relay, n_direct, n_near, _ = _engines(topo, routes[s])
+        to = [(wk, T.kd) for wk, _, _ in relays] + [(wv, T.vd) for _, wv, _ in relays]
+        g.wait_ge(sem.ld1, 32)
+        masks = _deal(topo, core, [(w, n_relay) for w, _ in to])
+        g.remote_dma_fused(
+            [RemoteDMATransfer(dst_ids=[_dst(topo, w, core)], dma_engine_mask=masks[w], remote_sem=sem.staged,
+                               src=piece[:, :], dst=piece[:, :]) for w, piece in to], local_sem=sem.sent)
+        g.wait_ge(sem.ld2, 32)
+        masks = _deal(topo, core, [(d, n_direct) for d in direct] + [(d, n_near) for d in near])
+        g.remote_dma_fused(
+            [RemoteDMATransfer(dst_ids=[_dst(topo, d, core)], dma_engine_mask=masks[d], remote_sem=sem["k%d" % s],
+                               src=T.kvd[:, :], dst=T.kv[:, W * s:W * s + W]) for d in direct + near], local_sem=sem.sent)
+        g.wait_ge(sem.sent, n_relay * len(to) + n_direct * len(direct) + n_near * len(near))
 
-    need = []
-    for s, (src, relays, near) in enumerate(routes):
+    need_k, need_v = [], []
+    for route in routes:
+        src, relays, direct, near = route
+        n = _engines(topo, route)
         if src == core:
-            need.append(32)
-        elif core in near:
-            need.append(_share(topo, src, [r for r, _ in relays] + near)[1])
+            need_k.append(16)
+            need_v.append(16)
+        elif core in direct or core in near:
+            need_k.append(n[1] if core in direct else n[2])
+            need_v.append(0)
         else:
-            need.append([_share(topo, w, ds)[1] for w, ds in relays if core in ds][0])
+            need_k.append(n[3])
+            need_v.append(n[3])
 
     pe, ve, ac = g.tensor, g.vector, g.scalar
     pe.wait_ge(sem.q, 32)
     pe.wait_ge(sem.qz0, 1)
     for s in range(2):
         k = T.kv[:, W * s:W * s + 128]
-        pe.wait_ge(sem["kv%d" % s], need[s])
+        pe.wait_ge(sem["k%d" % s], need_k[s])
         pe.matmul(T.ps_st[0:QP, 128 * s:128 * s + 128], T.qz[:, 0:QP], k, start=True, stop=True).then_inc(sem.st, 1)
         pe.matmul(T.ps_s[:, 0:2 * QP], k, T.qz[:, QP * s:QP * s + 2 * QP], start=(s == 0), stop=False).then_inc(sem.s, 1)
 
@@ -163,6 +181,8 @@ def rank_program(g, core, T, topo):
     for s in range(2):
         pe.matmul(T.ps_l[0:QP, 0:1], T.p[:, QP * s:QP * s + QP], T.ones[:, 0:1], start=(s == 0), stop=(s == 1)).then_inc(sem.l, 1)
     for s in range(2):
+        if need_v[s]:
+            pe.wait_ge(sem["v%d" % s], need_v[s])
         pe.matmul(T.ps_o[0:QP, 0:128], T.p[:, QP * s:QP * s + QP], T.kv[:, W * s + 128:W * s + W],
                   start=(s == 0), stop=(s == 1)).then_inc(sem.o, 1)
     ve.wait_ge(sem.l, 2)

@@ -4,28 +4,29 @@ from concourse.mybir import AluOpType, AxisListType, ActivationFunctionType
 SIM_CORES = 256
 QP = 32
 W = 256
+H = 64
 
 SCRATCH = {
     "kd": ("dram", [128, 128], "bfloat16"),
     "vd": ("dram", [128, 128], "bfloat16"),
     "kvd": ("dram", [128, W], "bfloat16"),
     "kv": ("sbuf", [128, 2 * W], "bfloat16"),
-    "qz": ("sbuf", [128, 3 * QP], "bfloat16"),
-    "zero": ("sbuf", [128, 128], "bfloat16"),
-    "ones": ("sbuf", [128, 128], "bfloat16"),
-    "eye2": ("sbuf", [128, 2 * QP], "bfloat16"),
-    "dg2": ("sbuf", [128, 2 * QP], "bfloat16"),
+    "q4": ("sbuf", [128, 4 * QP], "bfloat16"),
+    "zero": ("sbuf", [128, 8], "bfloat16"),
+    "ones": ("sbuf", [128, 8], "bfloat16"),
     "negm": ("sbuf", [128, 1], "float32"),
     "rl": ("sbuf", [128, 1], "float32"),
+    "pq": ("sbuf", [128, 2 * QP], "bfloat16"),
     "p": ("sbuf", [128, 2 * QP], "bfloat16"),
     "yt": ("sbuf", [128, 128], "bfloat16"),
     "ps_st": ("psum", [128, 512], "float32"),
-    "ps_s": ("psum", [128, 512], "float32"),
+    "ps_g": ("psum", [128, 512], "float32"),
     "ps_l": ("psum", [128, 512], "float32"),
-    "ps_o": ("psum", [128, 512], "float32"),
+    "ps_oa": ("psum", [128, 512], "float32"),
+    "ps_ob": ("psum", [128, 512], "float32"),
 }
-SEMAPHORES = ["ld1", "ld2", "staged", "sent", "k0", "k1", "v0", "v1", "q", "zero", "qz0", "eye1", "eye", "ones",
-              "st", "m", "dg", "s", "p", "l", "o", "rl", "y", "stored"]
+SEMAPHORES = ["ld1", "ld2", "staged", "sent", "k0", "k1", "v0", "v1", "q", "qc", "zero", "ones",
+              "st", "sg", "m", "e", "p", "l", "oa", "ob", "rl", "y", "stored"]
 
 
 def _place(topo, c):
@@ -105,26 +106,25 @@ def rank_program(g, core, T, topo):
         return
 
     own = [s for s, r in enumerate(routes) if r[0] == core]
+    pe, ve, ac = g.tensor, g.vector, g.scalar
 
     if own:
         g.sync.dma_start(T.kd[:, :], T.k[:, :]).then_inc(sem.ld1, 16)
         g.scalar.dma_start(T.vd[:, :], T.v[:, :]).then_inc(sem.ld1, 16)
         g.sync.dma_start(T.kvd[:, 0:128], T.k[:, :]).then_inc(sem.ld2, 16)
         g.scalar.dma_start(T.kvd[:, 128:W], T.v[:, :]).then_inc(sem.ld2, 16)
-    g.sync.dma_start(T.qz[:, 0:QP], T.q[:, :]).then_inc(sem.q, 16)
-    g.scalar.dma_start(T.qz[:, 2 * QP:3 * QP], T.q[:, :]).then_inc(sem.q, 16)
+    g.sync.dma_start(T.q4[:, 0:QP], T.q[:, :]).then_inc(sem.q, 16)
+    g.scalar.dma_start(T.q4[:, QP:2 * QP], T.q[:, :]).then_inc(sem.q, 16)
     if own:
         o = W * own[0]
         g.sync.dma_start(T.kv[:, o:o + 128], T.k[:, :]).then_inc(sem["k%d" % own[0]], 16)
         g.scalar.dma_start(T.kv[:, o + 128:o + W], T.v[:, :]).then_inc(sem["v%d" % own[0]], 16)
 
-    g.vector.memset(T.zero[:, :], 0.0).then_inc(sem.zero, 1)
-    g.vector.memset(T.eye2[0:QP, :], 1.0).then_inc(sem.eye1, 1)
-    g.vector.memset(T.qz[:, QP:2 * QP], 0.0).then_inc(sem.qz0, 1)
-    g.scalar.wait_ge(sem.zero, 1)
-    g.scalar.activation(T.ones[:, :], T.zero[:, :], ActivationFunctionType.Exp).then_inc(sem.ones, 1)
-    g.wait_ge(sem.eye1, 1)
-    g.affine_select(T.eye2[0:QP, :], T.eye2[0:QP, :], [[0, 2], [-1, QP]], AluOpType.is_equal, 0.0, 0, 1).then_inc(sem.eye, 1)
+    ve.memset(T.zero[:, :], 0.0).then_inc(sem.zero, 1)
+    ac.wait_ge(sem.zero, 1)
+    ac.activation(T.ones[:, :], T.zero[:, :], ActivationFunctionType.Exp).then_inc(sem.ones, 1)
+    ve.wait_ge(sem.q, 32)
+    ve.tensor_copy(T.q4[:, 2 * QP:4 * QP], T.q4[:, 0:2 * QP]).then_inc(sem.qc, 1)
 
     if own:
         s = own[0]
@@ -157,40 +157,45 @@ def rank_program(g, core, T, topo):
             need_k.append(n[3])
             need_v.append(n[3])
 
-    pe, ve, ac = g.tensor, g.vector, g.scalar
     pe.wait_ge(sem.q, 32)
-    pe.wait_ge(sem.qz0, 1)
+    pe.wait_ge(sem.qc, 1)
     for s in range(2):
-        k = T.kv[:, W * s:W * s + 128]
         pe.wait_ge(sem["k%d" % s], need_k[s])
-        pe.matmul(T.ps_st[0:QP, 128 * s:128 * s + 128], T.qz[:, 0:QP], k, start=True, stop=True).then_inc(sem.st, 1)
-        pe.matmul(T.ps_s[:, 0:2 * QP], k, T.qz[:, QP * s:QP * s + 2 * QP], start=(s == 0), stop=False).then_inc(sem.s, 1)
+        pe.matmul(T.ps_st[:, 128 * s:128 * s + 128], T.q4[:, :], T.kv[:, W * s:W * s + 128],
+                  start=True, stop=True).then_inc(sem.st, 1)
+    for s in range(2):
+        for a in range(4):
+            pe.matmul(T.ps_g[QP * a:QP * a + QP, QP * s:QP * s + QP], T.q4[:, 0:QP],
+                      T.kv[:, W * s + QP * a:W * s + QP * a + QP], start=True, stop=True).then_inc(sem.sg, 1)
 
     ve.wait_ge(sem.st, 2)
-    ve.tensor_reduce(T.negm[0:QP, 0:1], T.ps_st[0:QP, 0:256], AxisListType.X, AluOpType.max, negate=True).then_inc(sem.m, 1)
-    ve.wait_ge(sem.m, 1)
-    ve.wait_ge(sem.eye, 1)
-    ve.tensor_scalar(T.dg2[0:QP, :], T.eye2[0:QP, :], T.negm[0:QP, 0:1], None, AluOpType.mult).then_inc(sem.dg, 1)
+    ve.tensor_reduce(T.negm[:, 0:1], T.ps_st[:, 0:256], AxisListType.X, AluOpType.max, negate=True).then_inc(sem.m, 1)
+    ac.wait_ge(sem.m, 1)
+    ac.wait_ge(sem.sg, 8)
+    ac.activation(T.pq[:, :], T.ps_g[:, 0:2 * QP], ActivationFunctionType.Exp, bias=T.negm[:, 0:1]).then_inc(sem.e, 1)
+    ve.wait_ge(sem.e, 1)
+    ve.transpose(T.p[:, :], T.pq[:, :]).then_inc(sem.p, 1)
 
-    pe.wait_ge(sem.dg, 1)
-    pe.wait_ge(sem.ones, 1)
-    pe.matmul(T.ps_s[:, 0:2 * QP], T.ones[0:QP, 0:128], T.dg2[0:QP, :], start=False, stop=True).then_inc(sem.s, 1)
-    ac.wait_ge(sem.s, 3)
-    ac.activation(T.p[:, :], T.ps_s[:, 0:2 * QP], ActivationFunctionType.Exp).then_inc(sem.p, 1)
     pe.wait_ge(sem.p, 1)
+    pe.wait_ge(sem.ones, 1)
     for s in range(2):
         pe.matmul(T.ps_l[0:QP, 0:1], T.p[:, QP * s:QP * s + QP], T.ones[:, 0:1], start=(s == 0), stop=(s == 1)).then_inc(sem.l, 1)
     for s in range(2):
         if need_v[s]:
             pe.wait_ge(sem["v%d" % s], need_v[s])
-        pe.matmul(T.ps_o[0:QP, 0:128], T.p[:, QP * s:QP * s + QP], T.kv[:, W * s + 128:W * s + W],
-                  start=(s == 0), stop=(s == 1)).then_inc(sem.o, 1)
+    for bank, name, c in ((T.ps_oa, "oa", 0), (T.ps_ob, "ob", H)):
+        for s in range(2):
+            pe.matmul(bank[0:QP, 0:H], T.p[:, QP * s:QP * s + QP], T.kv[:, W * s + 128 + c:W * s + 128 + c + H],
+                      start=(s == 0), stop=(s == 1)).then_inc(sem[name], 1)
     ve.wait_ge(sem.l, 2)
     ve.reciprocal(T.rl[0:QP, 0:1], T.ps_l[0:QP, 0:1]).then_inc(sem.rl, 1)
     ve.wait_ge(sem.rl, 1)
-    ve.wait_ge(sem.o, 2)
-    ve.tensor_scalar(T.yt[0:QP, :], T.ps_o[0:QP, 0:128], T.rl[0:QP, 0:1], None, AluOpType.mult).then_inc(sem.y, 1)
+    ve.wait_ge(sem.oa, 2)
+    ve.tensor_scalar(T.yt[0:QP, 0:H], T.ps_oa[0:QP, 0:H], T.rl[0:QP, 0:1], None, AluOpType.mult).then_inc(sem.y, 1)
+    ac.wait_ge(sem.rl, 1)
+    ac.wait_ge(sem.ob, 2)
+    ac.activation(T.yt[0:QP, H:2 * H], T.ps_ob[0:QP, 0:H], ActivationFunctionType.Copy, scale=T.rl[0:QP, 0:1]).then_inc(sem.y, 1)
 
-    g.sync.wait_ge(sem.y, 1)
+    g.sync.wait_ge(sem.y, 2)
     g.sync.dma_start(T.y[:, :], T.yt[0:QP, :]).then_inc(sem.stored, 16)
     g.sync.wait_ge(sem.stored, 16)

from concourse.bass import DstId, RemoteDMATransfer
from concourse.mybir import AluOpType, AxisListType, ActivationFunctionType

SIM_CORES = 256
QP = 32
W = 256
H = 64

SCRATCH = {
    "kd": ("dram", [128, 128], "bfloat16"),
    "vd": ("dram", [128, 128], "bfloat16"),
    "kvd": ("dram", [128, W], "bfloat16"),
    "kv": ("sbuf", [128, 2 * W], "bfloat16"),
    "q4": ("sbuf", [128, 4 * QP], "bfloat16"),
    "zero": ("sbuf", [128, 8], "bfloat16"),
    "ones": ("sbuf", [128, 8], "bfloat16"),
    "negm": ("sbuf", [128, 1], "float32"),
    "rl": ("sbuf", [128, 1], "float32"),
    "pq": ("sbuf", [128, 2 * QP], "bfloat16"),
    "p": ("sbuf", [128, 2 * QP], "bfloat16"),
    "yt": ("sbuf", [128, 128], "bfloat16"),
    "ps_st": ("psum", [128, 512], "float32"),
    "ps_g": ("psum", [128, 512], "float32"),
    "ps_l": ("psum", [128, 512], "float32"),
    "ps_oa": ("psum", [128, 512], "float32"),
    "ps_ob": ("psum", [128, 512], "float32"),
}
SEMAPHORES = ["ld1", "ld2", "staged", "sent", "k0", "k1", "v0", "v1", "q", "qc", "zero", "ones",
              "st", "sg", "m", "e", "p", "l", "oa", "ob", "rl", "y", "stored"]


def _place(topo, c):
    return (topo.host(c), topo.chip(c))


def _count(mask):
    return bin(mask).count("1")


def _plan(T, topo):
    cores = list(T.cores)
    routes = []
    for j in T.tables["MEM"]:
        src = cores[j]
        idle = [w for w in range(SIM_CORES) if w not in cores and topo.die(w) == topo.die(src)]
        near = [d for d in cores if d != src and _place(topo, d) == _place(topo, src)]
        direct = [d for d in cores if _place(topo, d) != _place(topo, src) and topo.may_write(src, d)]
        far = {}
        for d in cores:
            if not topo.may_write(src, d):
                far.setdefault(_place(topo, d), []).append(d)
        relays = []
        for ds in far.values():
            able = [w for w in idle if all(topo.may_write(w, d) for d in ds)]
            wk = [w for w in able if _place(topo, w) == _place(topo, src)][0]
            wv = [w for w in able if all(topo.mates(w, d) for d in ds) and topo.may_write(src, w)][0]
            idle.remove(wk)
            idle.remove(wv)
            relays.append((wk, wv, ds))
        routes.append((src, relays, direct, near))
    return routes


def _engines(topo, route):
    src, relays, direct, near = route
    every = _count(topo.mask(src, near[0]))
    out = _count(topo.mask(src, direct[0]))
    wk, wv, ds = relays[0]
    return out // len(relays), out // len(direct), (every - out) // len(near), _count(topo.mask(wk, ds[0])) // len(ds)


def _deal(topo, src, wants):
    used, out = 0, {}
    for d, n in sorted(wants, key=lambda x: _count(topo.mask(src, x[0]))):
        m = topo.mask(src, d) & ~used
        bits = [1 << b for b in range(m.bit_length()) if (m >> b) & 1][0:n]
        out[d] = sum(bits)
        used |= out[d]
    return out


def _dst(topo, d, src):
    rid, pid = topo.addr(d, src)
    return DstId(rid=rid, pnc=pid)


def rank_program(g, core, T, topo):
    sem = T.sem
    routes = _plan(T, topo)

    for s, route in enumerate(routes):
        for wk, wv, ds in route[1]:
            if core not in (wk, wv):
                continue
            n = _engines(topo, route)
            piece, off, name = (T.kd, W * s, "k%d" % s) if core == wk else (T.vd, W * s + 128, "v%d" % s)
            g.wait_ge(sem.staged, n[0])
            masks = _deal(topo, core, [(d, n[3]) for d in ds])
            g.remote_dma_fused(
                [RemoteDMATransfer(dst_ids=[_dst(topo, d, core)], dma_engine_mask=masks[d], remote_sem=sem[name],
                                   src=piece[:, :], dst=T.kv[:, off:off + 128]) for d in ds], local_sem=sem.sent)
            g.wait_ge(sem.sent, n[3] * len(ds))
            return

    if T.rank_of(core) is None:
        return

    own = [s for s, r in enumerate(routes) if r[0] == core]
    pe, ve, ac = g.tensor, g.vector, g.scalar

    if own:
        g.sync.dma_start(T.kd[:, :], T.k[:, :]).then_inc(sem.ld1, 16)
        g.scalar.dma_start(T.vd[:, :], T.v[:, :]).then_inc(sem.ld1, 16)
        g.sync.dma_start(T.kvd[:, 0:128], T.k[:, :]).then_inc(sem.ld2, 16)
        g.scalar.dma_start(T.kvd[:, 128:W], T.v[:, :]).then_inc(sem.ld2, 16)
    g.sync.dma_start(T.q4[:, 0:QP], T.q[:, :]).then_inc(sem.q, 16)
    g.scalar.dma_start(T.q4[:, QP:2 * QP], T.q[:, :]).then_inc(sem.q, 16)
    if own:
        o = W * own[0]
        g.sync.dma_start(T.kv[:, o:o + 128], T.k[:, :]).then_inc(sem["k%d" % own[0]], 16)
        g.scalar.dma_start(T.kv[:, o + 128:o + W], T.v[:, :]).then_inc(sem["v%d" % own[0]], 16)

    ve.memset(T.zero[:, :], 0.0).then_inc(sem.zero, 1)
    ac.wait_ge(sem.zero, 1)
    ac.activation(T.ones[:, :], T.zero[:, :], ActivationFunctionType.Exp).then_inc(sem.ones, 1)
    ve.wait_ge(sem.q, 32)
    ve.tensor_copy(T.q4[:, 2 * QP:4 * QP], T.q4[:, 0:2 * QP]).then_inc(sem.qc, 1)

    if own:
        s = own[0]
        src, relays, direct, near = routes[s]
        n_relay, n_direct, n_near, _ = _engines(topo, routes[s])
        to = [(wk, T.kd) for wk, _, _ in relays] + [(wv, T.vd) for _, wv, _ in relays]
        g.wait_ge(sem.ld1, 32)
        masks = _deal(topo, core, [(w, n_relay) for w, _ in to])
        g.remote_dma_fused(
            [RemoteDMATransfer(dst_ids=[_dst(topo, w, core)], dma_engine_mask=masks[w], remote_sem=sem.staged,
                               src=piece[:, :], dst=piece[:, :]) for w, piece in to], local_sem=sem.sent)
        g.wait_ge(sem.ld2, 32)
        masks = _deal(topo, core, [(d, n_direct) for d in direct] + [(d, n_near) for d in near])
        g.remote_dma_fused(
            [RemoteDMATransfer(dst_ids=[_dst(topo, d, core)], dma_engine_mask=masks[d], remote_sem=sem["k%d" % s],
                               src=T.kvd[:, :], dst=T.kv[:, W * s:W * s + W]) for d in direct + near], local_sem=sem.sent)
        g.wait_ge(sem.sent, n_relay * len(to) + n_direct * len(direct) + n_near * len(near))

    need_k, need_v = [], []
    for route in routes:
        src, relays, direct, near = route
        n = _engines(topo, route)
        if src == core:
            need_k.append(16)
            need_v.append(16)
        elif core in direct or core in near:
            need_k.append(n[1] if core in direct else n[2])
            need_v.append(0)
        else:
            need_k.append(n[3])
            need_v.append(n[3])

    pe.wait_ge(sem.q, 32)
    pe.wait_ge(sem.qc, 1)
    for s in range(2):
        pe.wait_ge(sem["k%d" % s], need_k[s])
        pe.matmul(T.ps_st[:, 128 * s:128 * s + 128], T.q4[:, :], T.kv[:, W * s:W * s + 128],
                  start=True, stop=True).then_inc(sem.st, 1)
    for s in range(2):
        for a in range(4):
            pe.matmul(T.ps_g[QP * a:QP * a + QP, QP * s:QP * s + QP], T.q4[:, 0:QP],
                      T.kv[:, W * s + QP * a:W * s + QP * a + QP], start=True, stop=True).then_inc(sem.sg, 1)

    ve.wait_ge(sem.st, 2)
    ve.tensor_reduce(T.negm[:, 0:1], T.ps_st[:, 0:256], AxisListType.X, AluOpType.max, negate=True).then_inc(sem.m, 1)
    ac.wait_ge(sem.m, 1)
    ac.wait_ge(sem.sg, 8)
    ac.activation(T.pq[:, :], T.ps_g[:, 0:2 * QP], ActivationFunctionType.Exp, bias=T.negm[:, 0:1]).then_inc(sem.e, 1)
    ve.wait_ge(sem.e, 1)
    ve.transpose(T.p[:, :], T.pq[:, :]).then_inc(sem.p, 1)

    pe.wait_ge(sem.p, 1)
    pe.wait_ge(sem.ones, 1)
    for s in range(2):
        pe.matmul(T.ps_l[0:QP, 0:1], T.p[:, QP * s:QP * s + QP], T.ones[:, 0:1], start=(s == 0), stop=(s == 1)).then_inc(sem.l, 1)
    for s in range(2):
        if need_v[s]:
            pe.wait_ge(sem["v%d" % s], need_v[s])
    for bank, name, c in ((T.ps_oa, "oa", 0), (T.ps_ob, "ob", H)):
        for s in range(2):
            pe.matmul(bank[0:QP, 0:H], T.p[:, QP * s:QP * s + QP], T.kv[:, W * s + 128 + c:W * s + 128 + c + H],
                      start=(s == 0), stop=(s == 1)).then_inc(sem[name], 1)
    ve.wait_ge(sem.l, 2)
    ve.reciprocal(T.rl[0:QP, 0:1], T.ps_l[0:QP, 0:1]).then_inc(sem.rl, 1)
    ve.wait_ge(sem.rl, 1)
    ve.wait_ge(sem.oa, 2)
    ve.tensor_scalar(T.yt[0:QP, 0:H], T.ps_oa[0:QP, 0:H], T.rl[0:QP, 0:1], None, AluOpType.mult).then_inc(sem.y, 1)
    ac.wait_ge(sem.rl, 1)
    ac.wait_ge(sem.ob, 2)
    ac.activation(T.yt[0:QP, H:2 * H], T.ps_ob[0:QP, 0:H], ActivationFunctionType.Copy, scale=T.rl[0:QP, 0:1]).then_inc(sem.y, 1)

    g.sync.wait_ge(sem.y, 2)
    g.sync.dma_start(T.y[:, :], T.yt[0:QP, :]).then_inc(sem.stored, 16)
    g.sync.wait_ge(sem.stored, 16)
